import numpy as np
CORES = [4,5,6,7,0,1,2,3]
N = 8
def setup_inputs(rng):
    return {"x": rng.standard_normal((N, 128, 8), dtype=np.float32)}
def reference(x):
    s = x.sum(axis=0, dtype=np.float64).astype(x.dtype)
    b = 8 // N
    return {"y": np.stack([s[:, r * b:(r + 1) * b] for r in range(N)])}

@@ -1,0 +1,44 @@
+from concourse.bass import DstId, RemoteDMATransfer
+
+SCRATCH = {
+    "xs": ("sbuf", [128, 8], "float32"),
+    "land": ("sbuf", [128, 8], "float32"),
+    "res": ("sbuf", [128, 1], "float32"),
+}
+SEMAPHORES = ["loaded", "sent", "arrived", "folded", "stored"]
+
+
+def rank_program(g, core, T, topo):
+    k = T.rank_of(core)
+    if k is None:
+        return
+    n = len(T.cores)
+
+    def dst_id(rank):
+        rid, pid, _se = topo.addr(T.cores[rank])
+        return DstId(rid=rid, pnc=pid)
+
+    g.dma_start(T.xs[:], T.x[:]).then_inc(T.sem.loaded, 16)
+    g.wait_ge(T.sem.loaded, 16)
+
+    transfers = []
+    for r in range(n):
+        h = r ^ 1
+        if h == k:
+            continue
+        transfers.append(RemoteDMATransfer(
+            dst_ids=[dst_id(h)], dma_engine_mask=0x3 << (2 * len(transfers)), remote_sem=T.sem.arrived,
+            src=T.xs[:, r:r + 1], dst=T.land[:, k:k + 1], alu_op=0))
+    g.remote_dma_fused(transfers, local_sem=T.sem.sent)
+
+    g.wait_ge(T.sem.arrived, 2 * (n - 1))
+    o = k ^ 1
+    srcs = [T.xs[:, o:o + 1] if j == k else T.land[:, j:j + 1] for j in range(n)]
+    g.remote_dma_fused([RemoteDMATransfer(
+        dst_ids=[dst_id(o)], dma_engine_mask=0xFFFF, remote_sem=T.sem.folded,
+        srcs=srcs, dsts=[T.res[:]], alu_op=1)], local_sem=T.sem.sent)
+
+    g.wait_ge(T.sem.folded, 16)
+    g.dma_start(T.y[:], T.res[:]).then_inc(T.sem.stored, 16)
+    g.wait_ge(T.sem.stored, 16)
+    g.wait_ge(T.sem.sent, 2 * (n - 1) + 16)

@@ -1,11 +1,15 @@
 from concourse.bass import DstId, RemoteDMATransfer
+from concourse.mybir import AluOpType
 
 SCRATCH = {
     "xs": ("sbuf", [128, 8], "float32"),
     "land": ("sbuf", [128, 8], "float32"),
-    "res": ("sbuf", [128, 1], "float32"),
+    "res": ("dram", [128, 1], "float32"),
 }
-SEMAPHORES = ["loaded", "sent", "arrived", "folded", "stored"]
+SEMAPHORES = ["loaded", "seeded", "sent", "arrived", "folded", "stored"]
+
+COPY_ENGINES = 2
+FOLD_ENGINES = 16
 
 
 def rank_program(g, core, T, topo):
@@ -13,6 +17,7 @@ def rank_program(g, core, T, topo):
     if k is None:
         return
     n = len(T.cores)
+    o = k ^ 1
 
     def dst_id(rank):
         rid, pid, _se = topo.addr(T.cores[rank])
@@ -23,22 +28,23 @@ def rank_program(g, core, T, topo):
 
     transfers = []
     for r in range(n):
-        h = r ^ 1
-        if h == k:
+        if r == k or r == o:
             continue
+        mask = ((1 << COPY_ENGINES) - 1) << (COPY_ENGINES * len(transfers))
         transfers.append(RemoteDMATransfer(
-            dst_ids=[dst_id(h)], dma_engine_mask=0x3 << (2 * len(transfers)), remote_sem=T.sem.arrived,
+            dst_ids=[dst_id(r ^ 1)], dma_engine_mask=mask, remote_sem=T.sem.arrived,
             src=T.xs[:, r:r + 1], dst=T.land[:, k:k + 1], alu_op=0))
     g.remote_dma_fused(transfers, local_sem=T.sem.sent)
+    g.dma_start(T.y[:], T.xs[:, k:k + 1]).then_inc(T.sem.seeded, 16)
 
-    g.wait_ge(T.sem.arrived, 2 * (n - 1))
-    o = k ^ 1
-    srcs = [T.xs[:, o:o + 1] if j == k else T.land[:, j:j + 1] for j in range(n)]
+    g.wait_ge(T.sem.arrived, COPY_ENGINES * (n - 2))
+    srcs = [T.xs[:, o:o + 1] if j == k else T.land[:, j:j + 1] for j in range(n) if j != o]
     g.remote_dma_fused([RemoteDMATransfer(
-        dst_ids=[dst_id(o)], dma_engine_mask=0xFFFF, remote_sem=T.sem.folded,
+        dst_ids=[dst_id(o)], dma_engine_mask=(1 << FOLD_ENGINES) - 1, remote_sem=T.sem.folded,
         srcs=srcs, dsts=[T.res[:]], alu_op=1)], local_sem=T.sem.sent)
 
-    g.wait_ge(T.sem.folded, 16)
-    g.dma_start(T.y[:], T.res[:]).then_inc(T.sem.stored, 16)
+    g.wait_ge(T.sem.seeded, 16)
+    g.wait_ge(T.sem.folded, FOLD_ENGINES)
+    g.dma_start(T.y[:], T.res[:], accum_op=AluOpType.add).then_inc(T.sem.stored, 16)
     g.wait_ge(T.sem.stored, 16)
-    g.wait_ge(T.sem.sent, 2 * (n - 1) + 16)
+    g.wait_ge(T.sem.sent, COPY_ENGINES * (n - 2) + FOLD_ENGINES)

from concourse.bass import DstId, RemoteDMATransfer
from concourse.mybir import AluOpType

SCRATCH = {
    "xs": ("sbuf", [128, 8], "float32"),
    "land": ("sbuf", [128, 8], "float32"),
    "res": ("dram", [128, 1], "float32"),
}
SEMAPHORES = ["loaded", "seeded", "sent", "arrived", "folded", "stored"]

COPY_ENGINES = 2
FOLD_ENGINES = 16


def rank_program(g, core, T, topo):
    k = T.rank_of(core)
    if k is None:
        return
    n = len(T.cores)
    o = k ^ 1

    def dst_id(rank):
        rid, pid, _se = topo.addr(T.cores[rank])
        return DstId(rid=rid, pnc=pid)

    g.dma_start(T.xs[:], T.x[:]).then_inc(T.sem.loaded, 16)
    g.wait_ge(T.sem.loaded, 16)

    transfers = []
    for r in range(n):
        if r == k or r == o:
            continue
        mask = ((1 << COPY_ENGINES) - 1) << (COPY_ENGINES * len(transfers))
        transfers.append(RemoteDMATransfer(
            dst_ids=[dst_id(r ^ 1)], dma_engine_mask=mask, remote_sem=T.sem.arrived,
            src=T.xs[:, r:r + 1], dst=T.land[:, k:k + 1], alu_op=0))
    g.remote_dma_fused(transfers, local_sem=T.sem.sent)
    g.dma_start(T.y[:], T.xs[:, k:k + 1]).then_inc(T.sem.seeded, 16)

    g.wait_ge(T.sem.arrived, COPY_ENGINES * (n - 2))
    srcs = [T.xs[:, o:o + 1] if j == k else T.land[:, j:j + 1] for j in range(n) if j != o]
    g.remote_dma_fused([RemoteDMATransfer(
        dst_ids=[dst_id(o)], dma_engine_mask=(1 << FOLD_ENGINES) - 1, remote_sem=T.sem.folded,
        srcs=srcs, dsts=[T.res[:]], alu_op=1)], local_sem=T.sem.sent)

    g.wait_ge(T.sem.seeded, 16)
    g.wait_ge(T.sem.folded, FOLD_ENGINES)
    g.dma_start(T.y[:], T.res[:], accum_op=AluOpType.add).then_inc(T.sem.stored, 16)
    g.wait_ge(T.sem.stored, 16)
    g.wait_ge(T.sem.sent, COPY_ENGINES * (n - 2) + FOLD_ENGINES)
